import numpy as np
import ml_dtypes


def mxq(x, axis, fmt="e4m3"):
    dtype, down = {"e4m3": (ml_dtypes.float8_e4m3fn, 7), "e5m2": (ml_dtypes.float8_e5m2, 14)}[fmt]
    v = np.moveaxis(np.asarray(x, np.float32).astype(ml_dtypes.bfloat16).astype(np.float64), axis, -1)
    blocks = v.reshape(v.shape[:-1] + (-1, 32))
    amax = np.abs(blocks).max(-1, keepdims=True)
    byte = np.maximum(np.where(amax > 0, np.frexp(amax)[1] - 1 + 127, 0) - down, 1)
    scale = np.exp2(byte - 127.0)
    codes = (blocks / scale).astype(np.float32).astype(dtype).astype(np.float64)
    return np.moveaxis((codes * scale).reshape(v.shape), -1, axis)


WIDE = False


def mx_kscale(k):
    if not WIDE:
        return np.ones(k)
    levels = np.array([10, -10, 5, -5, 0])
    if k % 512:
        return np.exp2(np.random.permutation(np.resize(levels, k // 32))).repeat(32)
    a = np.empty((k // 512, 16))
    for p in range(k // 512):
        a[p, :8] = np.random.permutation(np.resize(levels, 8))
        for g in range(8):
            far = levels[np.abs(levels - a[p, g]) >= 10]
            a[p, g + 8] = far[np.random.randint(len(far))]
    return np.exp2(a.ravel()).repeat(32)


def f64(x):
    return np.asarray(x).astype(np.float64)


def striped(idx):
    return np.tile(idx.reshape(-1, 16).T, (8, 1)).astype(np.uint16)


def unstriped(offs):
    return offs[:16].T.reshape(-1).astype(np.int64)


E2M1 = np.array([0.0, 0.5, 1.0, 1.5, 2.0, 3.0, 4.0, 6.0, -0.0, -0.5, -1.0, -1.5, -2.0, -3.0, -4.0, -6.0])


def pack_weight(w, fmt):
    k, n = w.shape
    w = f64(np.asarray(w, np.float32).astype(ml_dtypes.bfloat16)).reshape(k // 32, 32, n)
    amax = np.abs(w).max(1)
    if fmt == "e4m3":
        byte = np.frexp(amax)[1] - 1 + 127 - 7
    else:
        mant, ex = np.frexp(amax / 6.0)
        byte = np.where(mant > 0.5, ex, ex - 1) + 127
    byte = np.clip(np.where(amax > 0, byte, 1), 1, 254)
    scaled = (w * np.exp2(127.0 - byte)[:, None, :]).reshape(k, n).astype(np.float32)
    by_word = np.ascontiguousarray(scaled.reshape(k // 512, 128, 4, n).transpose(0, 1, 3, 2))
    if fmt == "e4m3":
        words = by_word.astype(ml_dtypes.float8_e4m3fn).view(np.uint8)
    else:
        c = by_word.astype(ml_dtypes.float4_e2m1fn).view(np.uint8) & 0xF
        words = (c[..., 0::2] | (c[..., 1::2] << 4)).reshape(k // 512, 128, 2 * n)
    return np.ascontiguousarray(words), np.ascontiguousarray(byte.astype(np.uint8).reshape(k // 512, 16, n))


def unpack_weight(words, scales, fmt):
    g, _, n = scales.shape
    words = np.ascontiguousarray(words).reshape(g, 128, n, -1)
    if fmt == "e4m3":
        vals = words.view(ml_dtypes.float8_e4m3fn).astype(np.float64)
    else:
        nib = np.empty((g, 128, n, 4), np.uint8)
        nib[..., 0::2] = words & 0xF
        nib[..., 1::2] = words >> 4
        vals = E2M1[nib]
    vals = vals * np.repeat(np.exp2(scales.astype(np.float64) - 127.0), 8, axis=1)[..., None]
    return vals.transpose(0, 1, 3, 2).reshape(g * 512, n)


def silu(v):
    return v / (1.0 + np.exp(-np.maximum(v, -700.0)))


def d_silu(v):
    s = 1.0 / (1.0 + np.exp(-np.maximum(v, -700.0)))
    return s * (1.0 + v * (1.0 - s))


K, T, E, C, H, N = 256, 1280, 4, 256, 512, 512


def by_expert(wq, xq):
    return np.concatenate([wq[e].T @ xq[:, e * C:(e + 1) * C] for e in range(E)], axis=1)


def setup_inputs():
    n = np.random.standard_normal
    s = mx_kscale(N)[:, None]
    u = mx_kscale(H)
    w2 = [pack_weight(m, "e2m1") for m in n((E, N, H)) / np.sqrt(N) / s[None] * u[None, None, :]]
    w1 = [pack_weight(m, "e2m1") for m in n((E, H, K)) / np.sqrt(H) / u[None, :, None]]
    w3 = [pack_weight(m, "e2m1") for m in n((E, H, K)) / np.sqrt(H) / u[None, :, None]]
    return {
        "dyT": (n((N, T)) * s).astype(np.float32),
        "a1": n((H, E * C)).astype(np.float32),
        "a3": n((H, E * C)).astype(np.float32),
        "w2_words": np.stack([m[0] for m in w2]),
        "w2_scales": np.stack([m[1] for m in w2]),
        "w1_words": np.stack([m[0] for m in w1]),
        "w1_scales": np.stack([m[1] for m in w1]),
        "w3_words": np.stack([m[0] for m in w3]),
        "w3_scales": np.stack([m[1] for m in w3]),
        "gate": np.tile(np.random.uniform(0.2, 1.0, E * C), (N, 1)).astype(np.float32),
        "offs": striped(np.random.permutation(T)[:E * C]),
    }


def reference(dyT, a1, a3, w2_words, w2_scales, w1_words, w1_scales, w3_words, w3_scales, gate, offs):
    idx = unstriped(offs)
    w2 = np.stack([unpack_weight(w2_words[e], w2_scales[e], "e2m1") for e in range(E)])
    w1 = np.stack([unpack_weight(w1_words[e], w1_scales[e], "e2m1") for e in range(E)])
    w3 = np.stack([unpack_weight(w3_words[e], w3_scales[e], "e2m1") for e in range(E)])
    gq = mxq(f64(gate) * f64(dyT)[:, idx], 0, "e4m3")
    dh = by_expert(w2, gq)
    da1 = dh * f64(a3) * d_silu(f64(a1))
    da3 = dh * silu(f64(a1))
    dx = by_expert(w1, mxq(da1, 0, "e4m3")) + by_expert(w3, mxq(da3, 0, "e4m3"))
    out = np.zeros((K, T))
    out[:, idx] = dx
    return out

@@ -1,0 +1,267 @@
+from contextlib import ExitStack
+
+import concourse.mybir as mybir
+
+F32 = mybir.dt.float32
+BF16 = mybir.dt.bfloat16
+U32 = mybir.dt.uint32
+I32 = mybir.dt.int32
+U16 = mybir.dt.uint16
+U8 = mybir.dt.uint8
+FP8X4 = mybir.dt.float8_e4m3fn_x4
+FP4X4 = mybir.dt.float4_e2m1fn_x4
+ACT = mybir.ActivationFunctionType
+ALU = mybir.AluOpType
+
+P = 128
+PACK = 4
+N = 512
+H = 512
+K = 256
+T = 1280
+E = 4
+C = 256
+S = E * C
+HALF = 512
+CHUNK = 128
+ON_VECTOR = (3,)
+
+FLOPS = 2 * S * (N * H + 2 * H * K)
+BYTES = 4 * (N * T + 2 * H * S + K * T + S) + E * P * (2 * H + 4 * K) + E * 16 * (H + 2 * K) + 2 * 16 * S // 16
+
+
+def tile_moe_bdx_glu_silu_kernel(
+    tc, dyT, a1, a3, w2_words, w2_scales, w1_words, w1_scales, w3_words, w3_scales, gate, offs, out
+):
+    nc = tc.nc
+    with ExitStack() as ctx:
+        listp = ctx.enter_context(tc.tile_pool(name="listp", bufs=1))
+        keep = ctx.enter_context(tc.tile_pool(name="keep", bufs=1))
+        ring = ctx.enter_context(tc.tile_pool(name="ring", bufs=3))
+        psum = ctx.enter_context(tc.psum_pool(name="psum", bufs=1))
+
+        offsets = listp.tile([P, S // 16], U16, name="offsets")
+
+        planes = [keep.tile([P, T], F32, name=f"plane{t}") for t in range(PACK)]
+        gate_sb = keep.tile([P, S], F32, name="gate_sb")
+        a1_sb = keep.tile([P, PACK, S], F32, name="a1_sb")
+        a3_sb = keep.tile([P, PACK, S], F32, name="a3_sb")
+        h_sb = keep.tile([P, PACK, S], F32, name="h_sb")
+        s_sb = keep.tile([P, PACK, S], F32, name="s_sb")
+        p_sb = keep.tile([P, PACK, S], F32, name="p_sb")
+        w2_raw = keep.tile([P, E, 2 * H], U8, name="w2_raw", align_bytes=64)
+        w2_perm = keep.tile([P, E, 2 * H], U8, name="w2_perm", align_bytes=64)
+        w2s_raw = keep.tile([P, E, H], U8, name="w2s_raw", align_bytes=64)
+        w2s_perm = keep.tile([P, E, H], U8, name="w2s_perm", align_bytes=64)
+        w1_sb = keep.tile([P, E, 2 * K], U8, name="w1_sb", align_bytes=64)
+        w3_sb = keep.tile([P, E, 2 * K], U8, name="w3_sb", align_bytes=64)
+        w1s = keep.tile([P, E, K], U8, name="w1s", align_bytes=64)
+        w3s = keep.tile([P, E, K], U8, name="w3s", align_bytes=64)
+        win = [keep.tile([P, T], F32, name=f"win{b}") for b in range(K // P)]
+        warm = keep.tile([P, 1], F32, name="warm")
+
+        nc.vector.memset(w2s_raw[:].bitcast(I32), 0)
+        nc.vector.memset(warm[:], 0.0)
+        nc.scalar.activation(warm[:], warm[:], ACT.Silu)
+        nc.gpsimd.memset(w1s[:].bitcast(I32), 0)
+        nc.gpsimd.memset(w3s[:].bitcast(I32), 0)
+        for b in range(K // P):
+            nc.gpsimd.memset(win[b][:], 0.0)
+
+        w2_i = w2_words.bitcast(I32)
+        w1_i = w1_words.bitcast(I32)
+        w3_i = w3_words.bitcast(I32)
+
+        def load_words(tile, dram_i, e0, e1):
+            nc.sync.dma_start(
+                tile[:, e0:e1, :].bitcast(I32), dram_i[e0:e1, 0].rearrange("e p b -> p e b")
+            )
+
+        def load_scales(tile, dram):
+            for q in range(4):
+                nc.sync.dma_start(
+                    tile[32 * q : 32 * q + 4].bitcast(I32),
+                    dram.bitcast(I32)[:, 0, 4 * q : 4 * q + 4, :].rearrange("e f i -> f e i"),
+                )
+
+        dy4 = dyT.rearrange("(p j) t -> p j t", j=PACK)
+        a1_4 = a1.rearrange("(p j) s -> p j s", j=PACK)
+        a3_4 = a3.rearrange("(p j) s -> p j s", j=PACK)
+
+        halves = [slice(0, HALF), slice(HALF, 2 * HALF)]
+
+        def load_plane(t):
+            nc.sync.dma_start(planes[t][:], dy4[:, t, :])
+
+        def load_saved(tile, dram, e):
+            cols = slice(e * C, (e + 1) * C)
+            nc.sync.dma_start(tile[:, :, cols], dram[:, :, cols])
+
+        nc.sync.dma_start(offsets[:], offs)
+        nc.sync.dma_start(gate_sb[:, halves[0]], gate[0:P, halves[0]])
+        load_plane(0)
+        nc.sync.dma_start(gate_sb[:, halves[1]], gate[0:P, halves[1]])
+        load_saved(a1_sb, a1_4, 0)
+        load_plane(1)
+        load_plane(2)
+        load_plane(3)
+        load_saved(a1_sb, a1_4, 1)
+        load_scales(w2s_raw, w2_scales)
+        load_words(w2_raw, w2_i, 0, E)
+        load_saved(a3_sb, a3_4, 0)
+        load_saved(a3_sb, a3_4, 1)
+        load_saved(a1_sb, a1_4, 2)
+        load_words(w1_sb, w1_i, 0, E)
+        load_words(w3_sb, w3_i, 0, E)
+        load_scales(w1s, w1_scales)
+        load_scales(w3s, w3_scales)
+        load_saved(a3_sb, a3_4, 2)
+        load_saved(a1_sb, a1_4, 3)
+        load_saved(a3_sb, a3_4, 3)
+
+        def permute(e0, e1):
+            nc.vector.tensor_copy(
+                w2_perm[:, e0:e1, :].bitcast(U16).rearrange("p e (t m) -> p e t m", t=PACK),
+                w2_raw[:, e0:e1, :].bitcast(U16).rearrange("p e (m t) -> p e t m", t=PACK),
+            )
+
+        def permute_scales(e0, e1):
+            nc.vector.tensor_copy(
+                w2s_perm[:, e0:e1, :].rearrange("p e (t m) -> p e t m", t=PACK),
+                w2s_raw[:, e0:e1, :].rearrange("p e (m t) -> p e t m", t=PACK),
+            )
+
+        g_planes = [ring.tile([P, PACK, HALF], F32, name=f"g_planes{h}", bufs=1) for h in range(2)]
+
+        def gather(h, t):
+            nc.vector.tensor_tensor(
+                g_planes[h][:, t, :],
+                planes[t][:].indirect(offsets[:, h * 32 : (h + 1) * 32]),
+                gate_sb[:, halves[h]],
+                ALU.mult,
+            )
+
+        g_bf = [keep.tile([P, C, PACK], BF16, name=f"g_bf{e}", align_bytes=64) for e in range(E)]
+        g_codes = [keep.tile([P, C], U32, name=f"g_codes{e}", align_bytes=64) for e in range(E)]
+        g_scales = [keep.tile([P, C], U8, name=f"g_scales{e}", align_bytes=64) for e in range(E)]
+
+        def interleave(e):
+            src = g_planes[e // 2][:, :, (e % 2) * C : (e % 2 + 1) * C]
+            nc.scalar.activation(g_bf[e][:], src.rearrange("p j n -> p n j"), ACT.Copy)
+
+        def quantize_g(e):
+            nc.vector.quantize_mx(
+                out=g_codes[e][:].bitcast(FP8X4),
+                scales=g_scales[e][:],
+                in_=g_bf[e][:].rearrange("p n j -> p (n j)"),
+            )
+
+        def activations(e):
+            cols = slice(e * C, (e + 1) * C)
+            nc.scalar.activation(s_sb[:, :, cols], a1_sb[:, :, cols], ACT.Tanh, scale=0.5)
+            nc.scalar.activation(s_sb[:, :, cols], s_sb[:, :, cols], ACT.Copy, scale=0.5, bias=0.5)
+            nc.scalar.activation(p_sb[:, :, cols], a1_sb[:, :, cols], ACT.Silu, scale=-1.0)
+            if e not in ON_VECTOR:
+                nc.scalar.activation(p_sb[:, :, cols], p_sb[:, :, cols], ACT.Copy, scale=-1.0, bias=1.0)
+            nc.scalar.activation(h_sb[:, :, cols], a1_sb[:, :, cols], ACT.Silu)
+
+        def factors(e):
+            for c in range(2):
+                cols = slice(e * C + c * CHUNK, e * C + (c + 1) * CHUNK)
+                nc.gpsimd.tensor_tensor(a3_sb[:, :, cols], a3_sb[:, :, cols], s_sb[:, :, cols], ALU.mult)
+                if e in ON_VECTOR:
+                    nc.vector.scalar_tensor_tensor(
+                        a3_sb[:, :, cols], p_sb[:, :, cols], 1.0, a3_sb[:, :, cols], ALU.subtract, ALU.mult
+                    )
+                else:
+                    nc.gpsimd.tensor_tensor(a3_sb[:, :, cols], a3_sb[:, :, cols], p_sb[:, :, cols], ALU.mult)
+
+        da_bf = [ring.tile([P, 2, C, PACK], BF16, name=f"da_bf{e}", tag="da_bf", align_bytes=64) for e in range(E)]
+        da_codes = [ring.tile([P, 2, C], U32, name=f"da_codes{e}", tag="da_codes", align_bytes=64) for e in range(E)]
+        da_scales = [ring.tile([P, 2, C], U8, name=f"da_scales{e}", tag="da_scales", align_bytes=64) for e in range(E)]
+        dx_sb = [keep.tile([P, 2, C], F32, name=f"dx_sb{e}") for e in range(E)]
+
+        def hidden(e, c):
+            dh = psum.tile([P, PACK, CHUNK], F32, name="dh", bufs=5)
+            slots = slice(c * CHUNK, (c + 1) * CHUNK)
+            for t in range(PACK):
+                nc.tensor.matmul_mx(
+                    out=dh[:, t, :],
+                    lhsT=w2_perm[:, e, 2 * P * t : 2 * P * (t + 1)].bitcast(FP4X4),
+                    lhsT_scale=w2s_perm[:, e, P * t : P * (t + 1)],
+                    rhs=g_codes[e][:, slots].bitcast(FP8X4),
+                    rhs_scale=g_scales[e][:, slots],
+                    start=True,
+                    stop=True,
+                )
+            cols = slice(e * C + c * CHUNK, e * C + (c + 1) * CHUNK)
+            for i, factor in ((1, h_sb), (0, a3_sb)):
+                sign = -1.0 if i == 0 and e in ON_VECTOR else 1.0
+                nc.vector.scalar_tensor_tensor(
+                    da_bf[e][:, i, slots, :],
+                    dh[:].rearrange("p j n -> p n j"),
+                    sign,
+                    factor[:, :, cols].rearrange("p j n -> p n j"),
+                    ALU.mult,
+                    ALU.mult,
+                )
+
+        def quantize_da(e):
+            nc.vector.quantize_mx(
+                out=da_codes[e][:].rearrange("p i n -> p (i n)").bitcast(FP8X4),
+                scales=da_scales[e][:].rearrange("p i n -> p (i n)"),
+                in_=da_bf[e][:].rearrange("p i n j -> p (i n j)"),
+            )
+
+        def project(e):
+            dx = psum.tile([P, 2, C], F32, name="dx", bufs=3)
+            for b in range(2):
+                for c in range(2):
+                    slots = slice(c * CHUNK, (c + 1) * CHUNK)
+                    for i, (w, ws) in enumerate(((w1_sb, w1s), (w3_sb, w3s))):
+                        nc.tensor.matmul_mx(
+                            out=dx[:, b, slots],
+                            lhsT=w[:, e, 2 * P * b : 2 * P * (b + 1)].bitcast(FP4X4),
+                            lhsT_scale=ws[:, e, P * b : P * (b + 1)],
+                            rhs=da_codes[e][:, i, slots].bitcast(FP8X4),
+                            rhs_scale=da_scales[e][:, i, slots],
+                            start=(i == 0),
+                            stop=(i == 1),
+                        )
+            nc.scalar.copy(dx_sb[e][:], dx[:])
+
+        def scatter(e, b):
+            nc.vector.tensor_copy(win[b][:].indirect(offsets[:, e * 16 : (e + 1) * 16]), dx_sb[e][:, b, :])
+
+        for t in range(PACK):
+            gather(0, t)
+        permute_scales(0, E)
+        permute(0, E)
+        activations(0)
+        interleave(0)
+        interleave(1)
+        quantize_g(0)
+        quantize_g(1)
+        activations(1)
+        factors(0)
+        factors(1)
+        for t in range(PACK):
+            gather(1, t)
+        interleave(2)
+        interleave(3)
+        quantize_g(2)
+        quantize_g(3)
+        for e in range(E):
+            hidden(e, 0)
+            hidden(e, 1)
+            quantize_da(e)
+            project(e)
+            if e < 2:
+                activations(e + 2)
+                factors(e + 2)
+            if e > 0:
+                for b in range(2):
+                    scatter(e - 1, b)
+        for b in range(2):
+            scatter(E - 1, b)
+            nc.sync.dma_start(out[b * P : (b + 1) * P, :], win[b][:])

@@ -24,7 +24,8 @@ C = 256
 S = E * C
 HALF = 512
 CHUNK = 128
-ON_VECTOR = (3,)
+ON_VECTOR = (0, 1)
+DA3_ON_GPSIMD = (3,)
 
 FLOPS = 2 * S * (N * H + 2 * H * K)
 BYTES = 4 * (N * T + 2 * H * S + K * T + S) + E * P * (2 * H + 4 * K) + E * 16 * (H + 2 * K) + 2 * 16 * S // 16
@@ -66,7 +67,7 @@ def tile_moe_bdx_glu_silu_kernel(
         nc.gpsimd.memset(w1s[:].bitcast(I32), 0)
         nc.gpsimd.memset(w3s[:].bitcast(I32), 0)
         for b in range(K // P):
-            nc.gpsimd.memset(win[b][:], 0.0)
+            nc.vector.memset(win[b][:], 0.0)
 
         w2_i = w2_words.bitcast(I32)
         w1_i = w1_words.bitcast(I32)
@@ -77,9 +78,9 @@ def tile_moe_bdx_glu_silu_kernel(
                 tile[:, e0:e1, :].bitcast(I32), dram_i[e0:e1, 0].rearrange("e p b -> p e b")
             )
 
-        def load_scales(tile, dram):
+        def load_scales(queue, tile, dram):
             for q in range(4):
-                nc.sync.dma_start(
+                queue.dma_start(
                     tile[32 * q : 32 * q + 4].bitcast(I32),
                     dram.bitcast(I32)[:, 0, 4 * q : 4 * q + 4, :].rearrange("e f i -> f e i"),
                 )
@@ -99,25 +100,25 @@ def tile_moe_bdx_glu_silu_kernel(
 
         nc.sync.dma_start(offsets[:], offs)
         nc.sync.dma_start(gate_sb[:, halves[0]], gate[0:P, halves[0]])
+        load_scales(nc.sync, w2s_raw, w2_scales)
         load_plane(0)
-        nc.sync.dma_start(gate_sb[:, halves[1]], gate[0:P, halves[1]])
-        load_saved(a1_sb, a1_4, 0)
+        load_words(w2_raw, w2_i, 0, E)
         load_plane(1)
+        load_saved(a1_sb, a1_4, 0)
+        nc.sync.dma_start(gate_sb[:, halves[1]], gate[0:P, halves[1]])
         load_plane(2)
         load_plane(3)
         load_saved(a1_sb, a1_4, 1)
-        load_scales(w2s_raw, w2_scales)
-        load_words(w2_raw, w2_i, 0, E)
         load_saved(a3_sb, a3_4, 0)
-        load_saved(a3_sb, a3_4, 1)
         load_saved(a1_sb, a1_4, 2)
+        load_saved(a3_sb, a3_4, 2)
         load_words(w1_sb, w1_i, 0, E)
         load_words(w3_sb, w3_i, 0, E)
-        load_scales(w1s, w1_scales)
-        load_scales(w3s, w3_scales)
-        load_saved(a3_sb, a3_4, 2)
+        load_saved(a3_sb, a3_4, 1)
         load_saved(a1_sb, a1_4, 3)
         load_saved(a3_sb, a3_4, 3)
+        load_scales(nc.gpsimd, w1s, w1_scales)
+        load_scales(nc.gpsimd, w3s, w3_scales)
 
         def permute(e0, e1):
             nc.vector.tensor_copy(
@@ -159,22 +160,24 @@ def tile_moe_bdx_glu_silu_kernel(
         def activations(e):
             cols = slice(e * C, (e + 1) * C)
             nc.scalar.activation(s_sb[:, :, cols], a1_sb[:, :, cols], ACT.Tanh, scale=0.5)
-            nc.scalar.activation(s_sb[:, :, cols], s_sb[:, :, cols], ACT.Copy, scale=0.5, bias=0.5)
+            if e not in ON_VECTOR:
+                nc.scalar.activation(s_sb[:, :, cols], s_sb[:, :, cols], ACT.Copy, scale=0.5, bias=0.5)
             nc.scalar.activation(p_sb[:, :, cols], a1_sb[:, :, cols], ACT.Silu, scale=-1.0)
             if e not in ON_VECTOR:
                 nc.scalar.activation(p_sb[:, :, cols], p_sb[:, :, cols], ACT.Copy, scale=-1.0, bias=1.0)
             nc.scalar.activation(h_sb[:, :, cols], a1_sb[:, :, cols], ACT.Silu)
 
         def factors(e):
+            if e in ON_VECTOR:
+                cols = slice(e * C, (e + 1) * C)
+                a3_cols = a3_sb[:, :, cols]
+                nc.vector.scalar_tensor_tensor(a3_cols, s_sb[:, :, cols], 1.0, a3_cols, ALU.add, ALU.mult)
+                nc.vector.scalar_tensor_tensor(a3_cols, p_sb[:, :, cols], 1.0, a3_cols, ALU.subtract, ALU.mult)
+                return
             for c in range(2):
                 cols = slice(e * C + c * CHUNK, e * C + (c + 1) * CHUNK)
                 nc.gpsimd.tensor_tensor(a3_sb[:, :, cols], a3_sb[:, :, cols], s_sb[:, :, cols], ALU.mult)
-                if e in ON_VECTOR:
-                    nc.vector.scalar_tensor_tensor(
-                        a3_sb[:, :, cols], p_sb[:, :, cols], 1.0, a3_sb[:, :, cols], ALU.subtract, ALU.mult
-                    )
-                else:
-                    nc.gpsimd.tensor_tensor(a3_sb[:, :, cols], a3_sb[:, :, cols], p_sb[:, :, cols], ALU.mult)
+                nc.gpsimd.tensor_tensor(a3_sb[:, :, cols], a3_sb[:, :, cols], p_sb[:, :, cols], ALU.mult)
 
         da_bf = [ring.tile([P, 2, C, PACK], BF16, name=f"da_bf{e}", tag="da_bf", align_bytes=64) for e in range(E)]
         da_codes = [ring.tile([P, 2, C], U32, name=f"da_codes{e}", tag="da_codes", align_bytes=64) for e in range(E)]
@@ -196,12 +199,20 @@ def tile_moe_bdx_glu_silu_kernel(
                 )
             cols = slice(e * C + c * CHUNK, e * C + (c + 1) * CHUNK)
             for i, factor in ((1, h_sb), (0, a3_sb)):
-                sign = -1.0 if i == 0 and e in ON_VECTOR else 1.0
+                factor_nj = factor[:, :, cols].rearrange("p j n -> p n j")
+                if i == 1 and e in DA3_ON_GPSIMD:
+                    dh_sb = ring.tile([P, PACK, CHUNK], F32, name="dh_sb", bufs=2)
+                    nc.scalar.copy(dh_sb[:], dh[:])
+                    nc.gpsimd.tensor_tensor(
+                        da_bf[e][:, i, slots, :], dh_sb[:].rearrange("p j n -> p n j"), factor_nj, ALU.mult
+                    )
+                    continue
+                scale = -0.5 if i == 0 and e in ON_VECTOR else 1.0
                 nc.vector.scalar_tensor_tensor(
                     da_bf[e][:, i, slots, :],
                     dh[:].rearrange("p j n -> p n j"),
-                    sign,
-                    factor[:, :, cols].rearrange("p j n -> p n j"),
+                    scale,
+                    factor_nj,
                     ALU.mult,
                     ALU.mult,
                 )
@@ -233,18 +244,16 @@ def tile_moe_bdx_glu_silu_kernel(
         def scatter(e, b):
             nc.vector.tensor_copy(win[b][:].indirect(offsets[:, e * 16 : (e + 1) * 16]), dx_sb[e][:, b, :])
 
-        for t in range(PACK):
-            gather(0, t)
         permute_scales(0, E)
         permute(0, E)
-        activations(0)
+        for t in range(PACK):
+            gather(0, t)
         interleave(0)
+        activations(0)
         interleave(1)
         quantize_g(0)
         quantize_g(1)
         activations(1)
-        factors(0)
-        factors(1)
         for t in range(PACK):
             gather(1, t)
         interleave(2)
@@ -252,16 +261,18 @@ def tile_moe_bdx_glu_silu_kernel(
         quantize_g(2)
         quantize_g(3)
         for e in range(E):
+            factors(e)
             hidden(e, 0)
             hidden(e, 1)
             quantize_da(e)
             project(e)
             if e < 2:
                 activations(e + 2)
-                factors(e + 2)
-            if e > 0:
+            if e > 1:
                 for b in range(2):
-                    scatter(e - 1, b)
+                    scatter(e - 2, b)
+        scatter(2, 0)
+        scatter(2, 1)
         for b in range(2):
-            scatter(E - 1, b)
+            scatter(3, b)
             nc.sync.dma_start(out[b * P : (b + 1) * P, :], win[b][:])

@@ -148,7 +148,11 @@ def tile_moe_bdx_glu_silu_kernel(
 
         def interleave(e):
             src = g_planes[e // 2][:, :, (e % 2) * C : (e % 2 + 1) * C]
-            nc.scalar.activation(g_bf[e][:], src.rearrange("p j n -> p n j"), ACT.Copy)
+            nc.scalar.activation(
+                g_bf[e][:].rearrange("p (c i) j -> p c j i", i=4),
+                src.rearrange("p j (c i) -> p c j i", i=4),
+                ACT.Copy,
+            )
 
         def quantize_g(e):
             nc.vector.quantize_mx(
@@ -160,8 +164,8 @@ def tile_moe_bdx_glu_silu_kernel(
         def activations(e):
             cols = slice(e * C, (e + 1) * C)
             nc.scalar.activation(s_sb[:, :, cols], a1_sb[:, :, cols], ACT.Tanh, scale=0.5)
-            if e not in ON_VECTOR:
-                nc.scalar.activation(s_sb[:, :, cols], s_sb[:, :, cols], ACT.Copy, scale=0.5, bias=0.5)
+            sign = -0.5 if e in ON_VECTOR else 0.5
+            nc.scalar.activation(s_sb[:, :, cols], s_sb[:, :, cols], ACT.Copy, scale=sign, bias=sign)
             nc.scalar.activation(p_sb[:, :, cols], a1_sb[:, :, cols], ACT.Silu, scale=-1.0)
             if e not in ON_VECTOR:
                 nc.scalar.activation(p_sb[:, :, cols], p_sb[:, :, cols], ACT.Copy, scale=-1.0, bias=1.0)
@@ -171,7 +175,7 @@ def tile_moe_bdx_glu_silu_kernel(
             if e in ON_VECTOR:
                 cols = slice(e * C, (e + 1) * C)
                 a3_cols = a3_sb[:, :, cols]
-                nc.vector.scalar_tensor_tensor(a3_cols, s_sb[:, :, cols], 1.0, a3_cols, ALU.add, ALU.mult)
+                nc.vector.tensor_tensor(a3_cols, s_sb[:, :, cols], a3_cols, ALU.mult)
                 nc.vector.scalar_tensor_tensor(a3_cols, p_sb[:, :, cols], 1.0, a3_cols, ALU.subtract, ALU.mult)
                 return
             for c in range(2):
@@ -199,22 +203,17 @@ def tile_moe_bdx_glu_silu_kernel(
                 )
             cols = slice(e * C + c * CHUNK, e * C + (c + 1) * CHUNK)
             for i, factor in ((1, h_sb), (0, a3_sb)):
-                factor_nj = factor[:, :, cols].rearrange("p j n -> p n j")
+                factor_nj = factor[:, :, cols].rearrange("p j (c i) -> p c j i", i=4)
+                da_nj = da_bf[e][:, i, slots, :].rearrange("p (c i) j -> p c j i", i=4)
                 if i == 1 and e in DA3_ON_GPSIMD:
                     dh_sb = ring.tile([P, PACK, CHUNK], F32, name="dh_sb", bufs=2)
                     nc.scalar.copy(dh_sb[:], dh[:])
                     nc.gpsimd.tensor_tensor(
-                        da_bf[e][:, i, slots, :], dh_sb[:].rearrange("p j n -> p n j"), factor_nj, ALU.mult
+                        da_nj, dh_sb[:].rearrange("p j (c i) -> p c j i", i=4), factor_nj, ALU.mult
                     )
                     continue
-                scale = -0.5 if i == 0 and e in ON_VECTOR else 1.0
-                nc.vector.scalar_tensor_tensor(
-                    da_bf[e][:, i, slots, :],
-                    dh[:].rearrange("p j n -> p n j"),
-                    scale,
-                    factor_nj,
-                    ALU.mult,
-                    ALU.mult,
+                nc.vector.tensor_tensor(
+                    da_nj, dh[:].rearrange("p j (c i) -> p c j i", i=4), factor_nj, ALU.mult
                 )
 
         def quantize_da(e):

@@ -24,7 +24,7 @@ C = 256
 S = E * C
 HALF = 512
 CHUNK = 128
-ON_VECTOR = (0, 1)
+ON_VECTOR = (0,)
 DA3_ON_GPSIMD = (3,)
 
 FLOPS = 2 * S * (N * H + 2 * H * K)
@@ -99,26 +99,24 @@ def tile_moe_bdx_glu_silu_kernel(
             nc.sync.dma_start(tile[:, :, cols], dram[:, :, cols])
 
         nc.sync.dma_start(offsets[:], offs)
-        nc.sync.dma_start(gate_sb[:, halves[0]], gate[0:P, halves[0]])
         load_scales(nc.sync, w2s_raw, w2_scales)
+        nc.sync.dma_start(gate_sb[:, halves[0]], gate[0:P, halves[0]])
         load_plane(0)
-        load_words(w2_raw, w2_i, 0, E)
-        load_plane(1)
         load_saved(a1_sb, a1_4, 0)
         nc.sync.dma_start(gate_sb[:, halves[1]], gate[0:P, halves[1]])
+        load_plane(1)
+        load_words(w2_raw, w2_i, 0, E)
+        load_saved(a1_sb, a1_4, 1)
         load_plane(2)
         load_plane(3)
-        load_saved(a1_sb, a1_4, 1)
         load_saved(a3_sb, a3_4, 0)
-        load_saved(a1_sb, a1_4, 2)
-        load_saved(a3_sb, a3_4, 2)
+        load_saved(a3_sb, a3_4, 1)
+        nc.sync.dma_start(a1_sb[:, :, halves[1]], a1_4[:, :, halves[1]])
         load_words(w1_sb, w1_i, 0, E)
         load_words(w3_sb, w3_i, 0, E)
-        load_saved(a3_sb, a3_4, 1)
-        load_saved(a1_sb, a1_4, 3)
-        load_saved(a3_sb, a3_4, 3)
-        load_scales(nc.gpsimd, w1s, w1_scales)
-        load_scales(nc.gpsimd, w3s, w3_scales)
+        nc.sync.dma_start(a3_sb[:, :, halves[1]], a3_4[:, :, halves[1]])
+        load_scales(nc.sync, w1s, w1_scales)
+        load_scales(nc.sync, w3s, w3_scales)
 
         def permute(e0, e1):
             nc.vector.tensor_copy(
@@ -172,14 +170,16 @@ def tile_moe_bdx_glu_silu_kernel(
             nc.scalar.activation(h_sb[:, :, cols], a1_sb[:, :, cols], ACT.Silu)
 
         def factors(e):
+            chunks = [slice(e * C + c * CHUNK, e * C + (c + 1) * CHUNK) for c in range(2)]
             if e in ON_VECTOR:
-                cols = slice(e * C, (e + 1) * C)
-                a3_cols = a3_sb[:, :, cols]
-                nc.vector.tensor_tensor(a3_cols, s_sb[:, :, cols], a3_cols, ALU.mult)
-                nc.vector.scalar_tensor_tensor(a3_cols, p_sb[:, :, cols], 1.0, a3_cols, ALU.subtract, ALU.mult)
+                for cols in chunks:
+                    a3_cols = a3_sb[:, :, cols]
+                    nc.vector.tensor_tensor(a3_cols, s_sb[:, :, cols], a3_cols, ALU.mult)
+                for cols in chunks:
+                    a3_cols = a3_sb[:, :, cols]
+                    nc.vector.scalar_tensor_tensor(a3_cols, p_sb[:, :, cols], 1.0, a3_cols, ALU.subtract, ALU.mult)
                 return
-            for c in range(2):
-                cols = slice(e * C + c * CHUNK, e * C + (c + 1) * CHUNK)
+            for cols in chunks:
                 nc.gpsimd.tensor_tensor(a3_sb[:, :, cols], a3_sb[:, :, cols], s_sb[:, :, cols], ALU.mult)
                 nc.gpsimd.tensor_tensor(a3_sb[:, :, cols], a3_sb[:, :, cols], p_sb[:, :, cols], ALU.mult)
 
@@ -244,34 +244,54 @@ def tile_moe_bdx_glu_silu_kernel(
             nc.vector.tensor_copy(win[b][:].indirect(offsets[:, e * 16 : (e + 1) * 16]), dx_sb[e][:, b, :])
 
         permute_scales(0, E)
+        gather(0, 0)
+        gather(0, 1)
+        gather(0, 2)
+        gather(0, 3)
         permute(0, E)
-        for t in range(PACK):
-            gather(0, t)
         interleave(0)
         activations(0)
         interleave(1)
         quantize_g(0)
         quantize_g(1)
         activations(1)
-        for t in range(PACK):
-            gather(1, t)
+        gather(1, 0)
+        gather(1, 1)
+        gather(1, 2)
+        gather(1, 3)
         interleave(2)
         interleave(3)
         quantize_g(2)
         quantize_g(3)
-        for e in range(E):
-            factors(e)
-            hidden(e, 0)
-            hidden(e, 1)
-            quantize_da(e)
-            project(e)
-            if e < 2:
-                activations(e + 2)
-            if e > 1:
-                for b in range(2):
-                    scatter(e - 2, b)
+        factors(0)
+        hidden(0, 0)
+        hidden(0, 1)
+        quantize_da(0)
+        project(0)
+        activations(2)
+        factors(1)
+        hidden(1, 0)
+        hidden(1, 1)
+        scatter(0, 0)
+        quantize_da(1)
+        project(1)
+        activations(3)
+        scatter(0, 1)
+        factors(2)
+        hidden(2, 0)
+        hidden(2, 1)
+        scatter(1, 0)
+        quantize_da(2)
+        project(2)
+        scatter(1, 1)
+        factors(3)
+        hidden(3, 0)
+        hidden(3, 1)
         scatter(2, 0)
+        quantize_da(3)
+        project(3)
         scatter(2, 1)
-        for b in range(2):
-            scatter(3, b)
-            nc.sync.dma_start(out[b * P : (b + 1) * P, :], win[b][:])
+        scatter(3, 0)
+        nc.sync.dma_start(out[0 * P : (0 + 1) * P, :], win[0][:])
+        scatter(3, 1)
+        nc.sync.dma_start(out[1 * P : (1 + 1) * P, :], win[1][:])

from contextlib import ExitStack

import concourse.mybir as mybir

F32 = mybir.dt.float32
BF16 = mybir.dt.bfloat16
U32 = mybir.dt.uint32
I32 = mybir.dt.int32
U16 = mybir.dt.uint16
U8 = mybir.dt.uint8
FP8X4 = mybir.dt.float8_e4m3fn_x4
FP4X4 = mybir.dt.float4_e2m1fn_x4
ACT = mybir.ActivationFunctionType
ALU = mybir.AluOpType

P = 128
PACK = 4
N = 512
H = 512
K = 256
T = 1280
E = 4
C = 256
S = E * C
HALF = 512
CHUNK = 128
ON_VECTOR = (0,)
DA3_ON_GPSIMD = (3,)

FLOPS = 2 * S * (N * H + 2 * H * K)
BYTES = 4 * (N * T + 2 * H * S + K * T + S) + E * P * (2 * H + 4 * K) + E * 16 * (H + 2 * K) + 2 * 16 * S // 16


def tile_moe_bdx_glu_silu_kernel(
    tc, dyT, a1, a3, w2_words, w2_scales, w1_words, w1_scales, w3_words, w3_scales, gate, offs, out
):
    nc = tc.nc
    with ExitStack() as ctx:
        listp = ctx.enter_context(tc.tile_pool(name="listp", bufs=1))
        keep = ctx.enter_context(tc.tile_pool(name="keep", bufs=1))
        ring = ctx.enter_context(tc.tile_pool(name="ring", bufs=3))
        psum = ctx.enter_context(tc.psum_pool(name="psum", bufs=1))

        offsets = listp.tile([P, S // 16], U16, name="offsets")

        planes = [keep.tile([P, T], F32, name=f"plane{t}") for t in range(PACK)]
        gate_sb = keep.tile([P, S], F32, name="gate_sb")
        a1_sb = keep.tile([P, PACK, S], F32, name="a1_sb")
        a3_sb = keep.tile([P, PACK, S], F32, name="a3_sb")
        h_sb = keep.tile([P, PACK, S], F32, name="h_sb")
        s_sb = keep.tile([P, PACK, S], F32, name="s_sb")
        p_sb = keep.tile([P, PACK, S], F32, name="p_sb")
        w2_raw = keep.tile([P, E, 2 * H], U8, name="w2_raw", align_bytes=64)
        w2_perm = keep.tile([P, E, 2 * H], U8, name="w2_perm", align_bytes=64)
        w2s_raw = keep.tile([P, E, H], U8, name="w2s_raw", align_bytes=64)
        w2s_perm = keep.tile([P, E, H], U8, name="w2s_perm", align_bytes=64)
        w1_sb = keep.tile([P, E, 2 * K], U8, name="w1_sb", align_bytes=64)
        w3_sb = keep.tile([P, E, 2 * K], U8, name="w3_sb", align_bytes=64)
        w1s = keep.tile([P, E, K], U8, name="w1s", align_bytes=64)
        w3s = keep.tile([P, E, K], U8, name="w3s", align_bytes=64)
        win = [keep.tile([P, T], F32, name=f"win{b}") for b in range(K // P)]
        warm = keep.tile([P, 1], F32, name="warm")

        nc.vector.memset(w2s_raw[:].bitcast(I32), 0)
        nc.vector.memset(warm[:], 0.0)
        nc.scalar.activation(warm[:], warm[:], ACT.Silu)
        nc.gpsimd.memset(w1s[:].bitcast(I32), 0)
        nc.gpsimd.memset(w3s[:].bitcast(I32), 0)
        for b in range(K // P):
            nc.vector.memset(win[b][:], 0.0)

        w2_i = w2_words.bitcast(I32)
        w1_i = w1_words.bitcast(I32)
        w3_i = w3_words.bitcast(I32)

        def load_words(tile, dram_i, e0, e1):
            nc.sync.dma_start(
                tile[:, e0:e1, :].bitcast(I32), dram_i[e0:e1, 0].rearrange("e p b -> p e b")
            )

        def load_scales(queue, tile, dram):
            for q in range(4):
                queue.dma_start(
                    tile[32 * q : 32 * q + 4].bitcast(I32),
                    dram.bitcast(I32)[:, 0, 4 * q : 4 * q + 4, :].rearrange("e f i -> f e i"),
                )

        dy4 = dyT.rearrange("(p j) t -> p j t", j=PACK)
        a1_4 = a1.rearrange("(p j) s -> p j s", j=PACK)
        a3_4 = a3.rearrange("(p j) s -> p j s", j=PACK)

        halves = [slice(0, HALF), slice(HALF, 2 * HALF)]

        def load_plane(t):
            nc.sync.dma_start(planes[t][:], dy4[:, t, :])

        def load_saved(tile, dram, e):
            cols = slice(e * C, (e + 1) * C)
            nc.sync.dma_start(tile[:, :, cols], dram[:, :, cols])

        nc.sync.dma_start(offsets[:], offs)
        load_scales(nc.sync, w2s_raw, w2_scales)
        nc.sync.dma_start(gate_sb[:, halves[0]], gate[0:P, halves[0]])
        load_plane(0)
        load_saved(a1_sb, a1_4, 0)
        nc.sync.dma_start(gate_sb[:, halves[1]], gate[0:P, halves[1]])
        load_plane(1)
        load_words(w2_raw, w2_i, 0, E)
        load_saved(a1_sb, a1_4, 1)
        load_plane(2)
        load_plane(3)
        load_saved(a3_sb, a3_4, 0)
        load_saved(a3_sb, a3_4, 1)
        nc.sync.dma_start(a1_sb[:, :, halves[1]], a1_4[:, :, halves[1]])
        load_words(w1_sb, w1_i, 0, E)
        load_words(w3_sb, w3_i, 0, E)
        nc.sync.dma_start(a3_sb[:, :, halves[1]], a3_4[:, :, halves[1]])
        load_scales(nc.sync, w1s, w1_scales)
        load_scales(nc.sync, w3s, w3_scales)

        def permute(e0, e1):
            nc.vector.tensor_copy(
                w2_perm[:, e0:e1, :].bitcast(U16).rearrange("p e (t m) -> p e t m", t=PACK),
                w2_raw[:, e0:e1, :].bitcast(U16).rearrange("p e (m t) -> p e t m", t=PACK),
            )

        def permute_scales(e0, e1):
            nc.vector.tensor_copy(
                w2s_perm[:, e0:e1, :].rearrange("p e (t m) -> p e t m", t=PACK),
                w2s_raw[:, e0:e1, :].rearrange("p e (m t) -> p e t m", t=PACK),
            )

        g_planes = [ring.tile([P, PACK, HALF], F32, name=f"g_planes{h}", bufs=1) for h in range(2)]

        def gather(h, t):
            nc.vector.tensor_tensor(
                g_planes[h][:, t, :],
                planes[t][:].indirect(offsets[:, h * 32 : (h + 1) * 32]),
                gate_sb[:, halves[h]],
                ALU.mult,
            )

        g_bf = [keep.tile([P, C, PACK], BF16, name=f"g_bf{e}", align_bytes=64) for e in range(E)]
        g_codes = [keep.tile([P, C], U32, name=f"g_codes{e}", align_bytes=64) for e in range(E)]
        g_scales = [keep.tile([P, C], U8, name=f"g_scales{e}", align_bytes=64) for e in range(E)]

        def interleave(e):
            src = g_planes[e // 2][:, :, (e % 2) * C : (e % 2 + 1) * C]
            nc.scalar.activation(
                g_bf[e][:].rearrange("p (c i) j -> p c j i", i=4),
                src.rearrange("p j (c i) -> p c j i", i=4),
                ACT.Copy,
            )

        def quantize_g(e):
            nc.vector.quantize_mx(
                out=g_codes[e][:].bitcast(FP8X4),
                scales=g_scales[e][:],
                in_=g_bf[e][:].rearrange("p n j -> p (n j)"),
            )

        def activations(e):
            cols = slice(e * C, (e + 1) * C)
            nc.scalar.activation(s_sb[:, :, cols], a1_sb[:, :, cols], ACT.Tanh, scale=0.5)
            sign = -0.5 if e in ON_VECTOR else 0.5
            nc.scalar.activation(s_sb[:, :, cols], s_sb[:, :, cols], ACT.Copy, scale=sign, bias=sign)
            nc.scalar.activation(p_sb[:, :, cols], a1_sb[:, :, cols], ACT.Silu, scale=-1.0)
            if e not in ON_VECTOR:
                nc.scalar.activation(p_sb[:, :, cols], p_sb[:, :, cols], ACT.Copy, scale=-1.0, bias=1.0)
            nc.scalar.activation(h_sb[:, :, cols], a1_sb[:, :, cols], ACT.Silu)

        def factors(e):
            chunks = [slice(e * C + c * CHUNK, e * C + (c + 1) * CHUNK) for c in range(2)]
            if e in ON_VECTOR:
                for cols in chunks:
                    a3_cols = a3_sb[:, :, cols]
                    nc.vector.tensor_tensor(a3_cols, s_sb[:, :, cols], a3_cols, ALU.mult)
                for cols in chunks:
                    a3_cols = a3_sb[:, :, cols]
                    nc.vector.scalar_tensor_tensor(a3_cols, p_sb[:, :, cols], 1.0, a3_cols, ALU.subtract, ALU.mult)
                return
            for cols in chunks:
                nc.gpsimd.tensor_tensor(a3_sb[:, :, cols], a3_sb[:, :, cols], s_sb[:, :, cols], ALU.mult)
                nc.gpsimd.tensor_tensor(a3_sb[:, :, cols], a3_sb[:, :, cols], p_sb[:, :, cols], ALU.mult)

        da_bf = [ring.tile([P, 2, C, PACK], BF16, name=f"da_bf{e}", tag="da_bf", align_bytes=64) for e in range(E)]
        da_codes = [ring.tile([P, 2, C], U32, name=f"da_codes{e}", tag="da_codes", align_bytes=64) for e in range(E)]
        da_scales = [ring.tile([P, 2, C], U8, name=f"da_scales{e}", tag="da_scales", align_bytes=64) for e in range(E)]
        dx_sb = [keep.tile([P, 2, C], F32, name=f"dx_sb{e}") for e in range(E)]

        def hidden(e, c):
            dh = psum.tile([P, PACK, CHUNK], F32, name="dh", bufs=5)
            slots = slice(c * CHUNK, (c + 1) * CHUNK)
            for t in range(PACK):
                nc.tensor.matmul_mx(
                    out=dh[:, t, :],
                    lhsT=w2_perm[:, e, 2 * P * t : 2 * P * (t + 1)].bitcast(FP4X4),
                    lhsT_scale=w2s_perm[:, e, P * t : P * (t + 1)],
                    rhs=g_codes[e][:, slots].bitcast(FP8X4),
                    rhs_scale=g_scales[e][:, slots],
                    start=True,
                    stop=True,
                )
            cols = slice(e * C + c * CHUNK, e * C + (c + 1) * CHUNK)
            for i, factor in ((1, h_sb), (0, a3_sb)):
                factor_nj = factor[:, :, cols].rearrange("p j (c i) -> p c j i", i=4)
                da_nj = da_bf[e][:, i, slots, :].rearrange("p (c i) j -> p c j i", i=4)
                if i == 1 and e in DA3_ON_GPSIMD:
                    dh_sb = ring.tile([P, PACK, CHUNK], F32, name="dh_sb", bufs=2)
                    nc.scalar.copy(dh_sb[:], dh[:])
                    nc.gpsimd.tensor_tensor(
                        da_nj, dh_sb[:].rearrange("p j (c i) -> p c j i", i=4), factor_nj, ALU.mult
                    )
                    continue
                nc.vector.tensor_tensor(
                    da_nj, dh[:].rearrange("p j (c i) -> p c j i", i=4), factor_nj, ALU.mult
                )

        def quantize_da(e):
            nc.vector.quantize_mx(
                out=da_codes[e][:].rearrange("p i n -> p (i n)").bitcast(FP8X4),
                scales=da_scales[e][:].rearrange("p i n -> p (i n)"),
                in_=da_bf[e][:].rearrange("p i n j -> p (i n j)"),
            )

        def project(e):
            dx = psum.tile([P, 2, C], F32, name="dx", bufs=3)
            for b in range(2):
                for c in range(2):
                    slots = slice(c * CHUNK, (c + 1) * CHUNK)
                    for i, (w, ws) in enumerate(((w1_sb, w1s), (w3_sb, w3s))):
                        nc.tensor.matmul_mx(
                            out=dx[:, b, slots],
                            lhsT=w[:, e, 2 * P * b : 2 * P * (b + 1)].bitcast(FP4X4),
                            lhsT_scale=ws[:, e, P * b : P * (b + 1)],
                            rhs=da_codes[e][:, i, slots].bitcast(FP8X4),
                            rhs_scale=da_scales[e][:, i, slots],
                            start=(i == 0),
                            stop=(i == 1),
                        )
            nc.scalar.copy(dx_sb[e][:], dx[:])

        def scatter(e, b):
            nc.vector.tensor_copy(win[b][:].indirect(offsets[:, e * 16 : (e + 1) * 16]), dx_sb[e][:, b, :])

        permute_scales(0, E)
        gather(0, 0)
        gather(0, 1)
        gather(0, 2)
        gather(0, 3)
        permute(0, E)
        interleave(0)
        activations(0)
        interleave(1)
        quantize_g(0)
        quantize_g(1)
        activations(1)
        gather(1, 0)
        gather(1, 1)
        gather(1, 2)
        gather(1, 3)
        interleave(2)
        interleave(3)
        quantize_g(2)
        quantize_g(3)
        factors(0)
        hidden(0, 0)
        hidden(0, 1)
        quantize_da(0)
        project(0)
        activations(2)
        factors(1)
        hidden(1, 0)
        hidden(1, 1)
        scatter(0, 0)
        quantize_da(1)
        project(1)
        activations(3)
        scatter(0, 1)
        factors(2)
        hidden(2, 0)
        hidden(2, 1)
        scatter(1, 0)
        quantize_da(2)
        project(2)
        scatter(1, 1)
        factors(3)
        hidden(3, 0)
        hidden(3, 1)
        scatter(2, 0)
        quantize_da(3)
        project(3)
        scatter(2, 1)
        scatter(3, 0)
        nc.sync.dma_start(out[0 * P : (0 + 1) * P, :], win[0][:])
        scatter(3, 1)
        nc.sync.dma_start(out[1 * P : (1 + 1) * P, :], win[1][:])
